import numpy as np
import ml_dtypes


def mxq(x, axis, fmt="e4m3"):
    dtype, down = {"e4m3": (ml_dtypes.float8_e4m3fn, 7), "e5m2": (ml_dtypes.float8_e5m2, 14)}[fmt]
    v = np.moveaxis(np.asarray(x, np.float32).astype(ml_dtypes.bfloat16).astype(np.float64), axis, -1)
    blocks = v.reshape(v.shape[:-1] + (-1, 32))
    amax = np.abs(blocks).max(-1, keepdims=True)
    byte = np.maximum(np.where(amax > 0, np.frexp(amax)[1] - 1 + 127, 0) - down, 1)
    scale = np.exp2(byte - 127.0)
    codes = (blocks / scale).astype(np.float32).astype(dtype).astype(np.float64)
    return np.moveaxis((codes * scale).reshape(v.shape), -1, axis)


WIDE = False


def mx_kscale(k):
    if not WIDE:
        return np.ones(k)
    levels = np.array([10, -10, 5, -5, 0])
    if k % 512:
        return np.exp2(np.random.permutation(np.resize(levels, k // 32))).repeat(32)
    a = np.empty((k // 512, 16))
    for p in range(k // 512):
        a[p, :8] = np.random.permutation(np.resize(levels, 8))
        for g in range(8):
            far = levels[np.abs(levels - a[p, g]) >= 10]
            a[p, g + 8] = far[np.random.randint(len(far))]
    return np.exp2(a.ravel()).repeat(32)


def f64(x):
    return np.asarray(x).astype(np.float64)


def striped(idx):
    return np.tile(idx.reshape(-1, 16).T, (8, 1)).astype(np.uint16)


def unstriped(offs):
    return offs[:16].T.reshape(-1).astype(np.int64)


E2M1 = np.array([0.0, 0.5, 1.0, 1.5, 2.0, 3.0, 4.0, 6.0, -0.0, -0.5, -1.0, -1.5, -2.0, -3.0, -4.0, -6.0])


def pack_weight(w, fmt):
    k, n = w.shape
    w = f64(np.asarray(w, np.float32).astype(ml_dtypes.bfloat16)).reshape(k // 32, 32, n)
    amax = np.abs(w).max(1)
    if fmt == "e4m3":
        byte = np.frexp(amax)[1] - 1 + 127 - 7
    else:
        mant, ex = np.frexp(amax / 6.0)
        byte = np.where(mant > 0.5, ex, ex - 1) + 127
    byte = np.clip(np.where(amax > 0, byte, 1), 1, 254)
    scaled = (w * np.exp2(127.0 - byte)[:, None, :]).reshape(k, n).astype(np.float32)
    by_word = np.ascontiguousarray(scaled.reshape(k // 512, 128, 4, n).transpose(0, 1, 3, 2))
    if fmt == "e4m3":
        words = by_word.astype(ml_dtypes.float8_e4m3fn).view(np.uint8)
    else:
        c = by_word.astype(ml_dtypes.float4_e2m1fn).view(np.uint8) & 0xF
        words = (c[..., 0::2] | (c[..., 1::2] << 4)).reshape(k // 512, 128, 2 * n)
    return np.ascontiguousarray(words), np.ascontiguousarray(byte.astype(np.uint8).reshape(k // 512, 16, n))


def unpack_weight(words, scales, fmt):
    g, _, n = scales.shape
    words = np.ascontiguousarray(words).reshape(g, 128, n, -1)
    if fmt == "e4m3":
        vals = words.view(ml_dtypes.float8_e4m3fn).astype(np.float64)
    else:
        nib = np.empty((g, 128, n, 4), np.uint8)
        nib[..., 0::2] = words & 0xF
        nib[..., 1::2] = words >> 4
        vals = E2M1[nib]
    vals = vals * np.repeat(np.exp2(scales.astype(np.float64) - 127.0), 8, axis=1)[..., None]
    return vals.transpose(0, 1, 3, 2).reshape(g * 512, n)


def gelu(v):
    return 0.5 * v * (1.0 + np.tanh(np.sqrt(2.0 / np.pi) * (v + 0.044715 * v**3)))


def striped8(idx):
    return np.concatenate([v.reshape(-1, 16).T for v in idx]).astype(np.uint16)


def unstriped8(offs):
    return np.stack([offs[16 * g:16 * g + 16].T.reshape(-1) for g in range(8)]).astype(np.int64)


def heads(h, wgt, idx8):
    r = np.arange(h.shape[0])
    return wgt[r // 4 % 128] * h[r[:, None], idx8[r % 512 // 64]]


K, T, H, S, P, N = 1024, 2048, 1024, 1024, 512, 512

def setup_inputs():
    n = np.random.standard_normal
    s = mx_kscale(K)[:, None]
    u = mx_kscale(H)[:, None]
    tab_words, tab_scales = pack_weight(n((K, T)) * s, "e4m3")
    w1_words, w1_scales = pack_weight(n((K, H)) * 1.2 / np.sqrt(K) / s, "e2m1")
    w4_words, w4_scales = pack_weight(n((H, N)) / np.sqrt(H) / u, "e4m3")
    return {
        "tab_words": tab_words, "tab_scales": tab_scales,
        "offs": striped(np.random.permutation(T)[:S]),
        "offs2": striped8(np.stack([np.random.permutation(S)[:P] for _ in range(8)])),
        "offs3": striped8(np.stack([np.random.permutation(S)[:P] for _ in range(8)])),
        "w1_words": w1_words, "w1_scales": w1_scales,
        "w2": (n((K, H)) * 0.5 / np.sqrt(K) / s).astype(np.float32),
        "gain": (np.random.uniform(0.5, 1.5, H) * u[:, 0]).astype(np.float32),
        "wga": np.repeat(np.random.uniform(0.5, 2.0, (8, P)), 16, axis=0).astype(np.float32),
        "wgb": np.repeat(np.random.uniform(0.5, 2.0, (8, P)), 16, axis=0).astype(np.float32),
        "w3": (n((H, N)) * 1.1 / np.sqrt(H) / u).astype(np.float32),
        "w4_words": w4_words, "w4_scales": w4_scales,
    }

def reference(tab_words, tab_scales, offs, offs2, offs3, w1_words, w1_scales, w2, gain, wga, wgb, w3, w4_words, w4_scales):
    v = unpack_weight(tab_words, tab_scales, "e4m3")[:, unstriped(offs)]
    w1 = unpack_weight(w1_words, w1_scales, "e2m1")
    w4 = unpack_weight(w4_words, w4_scales, "e4m3")
    a1 = w1.T @ v
    a2 = mxq(f64(w2), 0, "e4m3").T @ v
    h = f64(gain)[:, None] * (np.tanh(a1) + np.cos(a2))
    xa = heads(h, f64(wga), unstriped8(offs2))
    xb = heads(h, f64(wgb), unstriped8(offs3))
    z = mxq(np.minimum(xa, xb), 0, "e4m3")
    y1 = mxq(f64(w3), 0, "e4m3").T @ z
    y2 = w4.T @ z
    return np.tanh(y1) * np.exp(-np.abs(y2))

@@ -1,0 +1,298 @@
+from contextlib import ExitStack
+
+import concourse.mybir as mybir
+
+K, T, H, S, M, N = 1024, 2048, 1024, 1024, 512, 512
+FLOPS = 2 * (2 * K * H * S + 2 * H * N * M)
+
+F32 = mybir.dt.float32
+BF16 = mybir.dt.bfloat16
+I32 = mybir.dt.int32
+U32 = mybir.dt.uint32
+U16 = mybir.dt.uint16
+U8 = mybir.dt.uint8
+FP8X4 = mybir.dt.float8_e4m3fn_x4
+FP4X4 = mybir.dt.float4_e2m1fn_x4
+ALU = mybir.AluOpType
+ACT = mybir.ActivationFunctionType
+
+P = 128
+PASS = 512
+BANK = 512
+LAST_SLICES = ((0, 256), (256, 128), (384, 128))
+GAIN_ON_VECTOR = 8
+
+
+def tile_list_antivenom_panel_features_kernel(
+    tc, tab_words, tab_scales, offs, offs2, offs3, w1_words, w1_scales, w2, gain, wga, wgb, w3, w4_words, w4_scales, out
+):
+    nc = tc.nc
+    with ExitStack() as ctx:
+        keep = ctx.enter_context(tc.tile_pool(name="keep", bufs=1))
+        work = ctx.enter_context(tc.tile_pool(name="work", bufs=2))
+        psum = ctx.enter_context(tc.psum_pool(name="psum", bufs=8))
+
+        def held(shape, dtype, name):
+            return keep.tile(shape, dtype, name=name, align_bytes=64)
+
+        list_v = keep.tile([P, S // 16], U16, name="list_v")
+        list_a = keep.tile([P, M // 16], U16, name="list_a")
+        list_b = keep.tile([P, M // 16], U16, name="list_b")
+        tab = [held([P, T], U32, f"tab{a}") for a in range(2)]
+        tab_sc = held([P, T], U8, "tab_sc")
+        v_sc = [held([P, S], U8, f"v_sc{a}") for a in range(2)]
+        v_words = [[held([P, BANK], U32, f"v_words{a}{half}") for half in range(2)] for a in range(2)]
+        w1_raw = [held([P, 2, 2 * PASS], U8, f"w1_raw{b}") for b in range(2)]
+        w1_codes = [held([P, 2, 2 * PASS], U8, f"w1_codes{b}") for b in range(2)]
+        w1_sc_raw = held([P, 2, H], U8, "w1_sc_raw")
+        w1_sc = [held([P, 2, PASS], U8, f"w1_sc{b}") for b in range(2)]
+        w2_codes = [[held([P, PASS], U32, f"w2_codes{a}{b}") for b in range(2)] for a in range(2)]
+        w2_sc = [[held([P, PASS], U8, f"w2_sc{a}{b}") for b in range(2)] for a in range(2)]
+        w3_codes = [held([P, N], U32, f"w3_codes{b}") for b in range(2)]
+        w3_sc = [held([P, N], U8, f"w3_sc{b}") for b in range(2)]
+        w4_codes = held([P, 2, N], U32, "w4_codes")
+        w4_sc = held([P, N], U8, "w4_sc")
+        g = held([P, 2, 4], F32, "g")
+        g_neg2 = held([P, 2, 4], F32, "g_neg2")
+        wa = held([P, M], F32, "wa")
+        wb = held([P, M], F32, "wb")
+        zero_in = held([P, 1], F32, "zero_in")
+        zero = held([P, 1], F32, "zero")
+
+        nc.vector.memset(zero_in[:], 0.0)
+        nc.scalar.activation(out=zero[:], in_=zero_in[:], func=ACT.Silu)
+        nc.vector.memset(tab_sc[:].bitcast(I32), 0)
+        nc.vector.memset(w1_sc_raw[:].bitcast(I32), 0)
+        nc.vector.memset(v_sc[1][:].bitcast(I32), 0)
+        nc.vector.memset(w4_sc[:].bitcast(I32), 0)
+
+        def load_rows(w, a, cols):
+            raw = work.tile([P, 4, PASS], F32, name="raw", bufs=4)
+            nc.sync.dma_start(out=raw[:], in_=w[PASS * a : PASS * (a + 1), cols].rearrange("(p j) c -> p j c", j=4))
+            return raw
+
+        def load_w1(b):
+            src = w1_words[:, :, 2 * PASS * b : 2 * PASS * (b + 1)].rearrange("a p n -> p a n")
+            nc.sync.dma_start(out=w1_raw[b][:].bitcast(I32), in_=src.bitcast(I32))
+
+        def load_table(a):
+            nc.sync.dma_start(out=tab[a][:].bitcast(I32), in_=tab_words[a].rearrange("p t i -> p (t i)").bitcast(I32))
+
+        def load_packed_scales(plane, scales):
+            for quad in range(4):
+                nc.sync.dma_start(
+                    out=plane[32 * quad : 32 * quad + 8, :].bitcast(I32),
+                    in_=scales[:, 4 * quad : 4 * quad + 4, :].bitcast(I32),
+                )
+
+        nc.sync.dma_start(list_v[:], offs)
+        w2_raw = {(0, 0): load_rows(w2, 0, slice(0, PASS))}
+        load_packed_scales(tab_sc, tab_scales)
+        for quad in range(4):
+            nc.sync.dma_start(
+                out=w1_sc_raw[32 * quad : 32 * quad + 4, :, :].bitcast(I32),
+                in_=w1_scales[:, 4 * quad : 4 * quad + 4, :].rearrange("a r n -> r a n").bitcast(I32),
+            )
+        w2_raw[1, 0] = load_rows(w2, 1, slice(0, PASS))
+        load_w1(0)
+        load_table(0)
+        load_table(1)
+        nc.sync.dma_start(out=g[:], in_=gain.rearrange("(b p i) -> p b i", b=2, i=4))
+        nc.sync.dma_start(list_a[:], offs2)
+        nc.sync.dma_start(list_b[:], offs3)
+        nc.sync.dma_start(out=wa[:], in_=wga)
+        nc.sync.dma_start(out=wb[:], in_=wgb)
+        load_w1(1)
+        for a in range(2):
+            w2_raw[a, 1] = load_rows(w2, a, slice(PASS, 2 * PASS))
+        w3_raw = [load_rows(w3, b, slice(0, N)) for b in range(2)]
+        nc.sync.dma_start(out=w4_codes[:].bitcast(I32), in_=w4_words.rearrange("a p c i -> p a (c i)").bitcast(I32))
+        load_packed_scales(w4_sc, w4_scales)
+
+        def deal_w1_scales(b):
+            nc.vector.tensor_copy(
+                out=w1_sc[b][:].rearrange("p a (t q) -> p a t q", t=4),
+                in_=w1_sc_raw[:, :, PASS * b : PASS * (b + 1)].rearrange("p a (q t) -> p a t q", t=4),
+            )
+
+        def deal_w1(b):
+            nc.scalar.copy(
+                out=w1_codes[b][:].bitcast(U16).rearrange("p a (t q) -> p a t q", t=4),
+                in_=w1_raw[b][:].bitcast(U16).rearrange("p a (q t) -> p a t q", t=4),
+            )
+
+        def gather_words(a, half):
+            cols = slice(half * BANK // 16, (half + 1) * BANK // 16)
+            nc.vector.tensor_copy(out=v_words[a][half][:], in_=tab[a][:].indirect(list_v[:, cols]))
+
+        def round_w2(copy, a, b):
+            grouped = work.tile([P, 4, P, 4], BF16, name="grouped", align_bytes=64)
+            copy(
+                out=grouped[:].rearrange("p t q j -> p q j t"),
+                in_=w2_raw[a, b][:].rearrange("p j (q t) -> p q j t", t=4),
+            )
+            return grouped[:].rearrange("p t q j -> p (t q j)")
+
+        def round_w3(b):
+            grouped = work.tile([P, N, 4], BF16, name="grouped", align_bytes=64)
+            nc.scalar.copy(
+                out=grouped[:].rearrange("p (c k) j -> p c j k", k=4),
+                in_=w3_raw[b][:].rearrange("p j (c k) -> p c j k", k=4),
+            )
+            return grouped[:].rearrange("p c j -> p (c j)")
+
+        def quantize(codes, scales, values):
+            nc.vector.quantize_mx(out=codes.bitcast(FP8X4), scales=scales, in_=values)
+
+        rounded = [round_w2(nc.scalar.copy, a, 0) for a in range(2)]
+        deal_w1(0)
+        nc.vector.tensor_copy(out=v_sc[0][:], in_=tab_sc[:].indirect(list_v[:]))
+        nc.gpsimd.dma_start(out=v_sc[1][0 : P - 4, :].bitcast(I32), in_=v_sc[0][4:P, :].bitcast(I32))
+        for b in range(2):
+            deal_w1_scales(b)
+        quantize(w2_codes[0][0][:], w2_sc[0][0][:], rounded[0])
+        gather_words(0, 0)
+        gather_words(0, 1)
+        quantize(w2_codes[1][0][:], w2_sc[1][0][:], rounded[1])
+        gather_words(1, 0)
+        gather_words(1, 1)
+        nc.vector.tensor_scalar(out=g_neg2[:], in0=g[:], scalar1=-2.0, scalar2=None, op0=ALU.mult)
+
+        def first_product(half, stationary):
+            bank = psum.tile([P, BANK], F32, name="bank")
+            cols = slice(half * BANK, (half + 1) * BANK)
+            for a in range(2):
+                codes, scales = stationary(a)
+                nc.tensor.matmul_mx(
+                    out=bank[:],
+                    lhsT=codes,
+                    lhsT_scale=scales,
+                    rhs=v_words[a][half][:].bitcast(FP8X4),
+                    rhs_scale=v_sc[a][:, cols],
+                    start=(a == 0),
+                    stop=(a == 1),
+                )
+            return bank
+
+        def features(b, i):
+            th = work.tile([P, S], F32, name="th", bufs=3)
+            sn = work.tile([P, S], F32, name="sn")
+            rows = slice(P * i, P * (i + 1))
+            for half in range(2):
+                cols = slice(half * BANK, (half + 1) * BANK)
+                a1 = first_product(
+                    half,
+                    lambda a: (w1_codes[b][:, a, 2 * P * i : 2 * P * (i + 1)].bitcast(FP4X4), w1_sc[b][:, a, rows]),
+                )
+                nc.scalar.activation(out=th[:, cols], in_=a1[:], func=ACT.Tanh, bias=zero[:])
+            for half in range(2):
+                cols = slice(half * BANK, (half + 1) * BANK)
+                a2 = first_product(half, lambda a: (w2_codes[a][b][:, rows].bitcast(FP8X4), w2_sc[a][b][:, rows]))
+                nc.scalar.activation(out=sn[:, cols], in_=a2[:], func=ACT.Sin, bias=zero[:], scale=0.5)
+            sq = work.tile([P, S], F32, name="sq", bufs=2)
+            nc.scalar.activation(out=sq[:], in_=sn[:], func=ACT.Square, bias=zero[:])
+            gi = g[:, b, i : i + 1]
+            h = work.tile([P, S], F32, name="h", bufs=5)
+            part = work.tile([P, S], F32, name="part", bufs=3)
+            if 4 * b + i < GAIN_ON_VECTOR:
+                nc.vector.scalar_tensor_tensor(
+                    out=part[:], in0=sq[:], scalar=-2.0, in1=th[:], op0=ALU.mult, op1=ALU.add
+                )
+                nc.vector.tensor_scalar(out=h[:], in0=part[:], scalar1=1.0, scalar2=gi, op0=ALU.add, op1=ALU.mult)
+            else:
+                nc.scalar.activation(
+                    out=part[:], in_=sq[:], func=ACT.Identity, bias=gi, scale=g_neg2[:, b, i : i + 1]
+                )
+                nc.vector.scalar_tensor_tensor(out=h[:], in0=th[:], scalar=gi, in1=part[:], op0=ALU.mult, op1=ALU.add)
+            return h
+
+        def picked_tiles(width):
+            xa = work.tile([P, 4, width], F32, name="xa", bufs=1)
+            xb = work.tile([P, 4, width], F32, name="xb", bufs=1)
+            return xa, xb
+
+        def pick(h, xa, xb, i, m0, width):
+            cols = slice(m0 // 16, (m0 + width) // 16)
+            for x, offsets, weight in ((xa, list_a, wa), (xb, list_b, wb)):
+                nc.vector.tensor_tensor(
+                    out=x[:, i, :], in0=h[:].indirect(offsets[:, cols]), in1=weight[:, m0 : m0 + width], op=ALU.mult
+                )
+
+        def smaller(xa, xb, width, name):
+            z = keep.tile([P, width, 4], BF16, name=f"z{name}", align_bytes=64)
+            nc.vector.tensor_tensor(
+                out=z[:].rearrange("p (c k) i -> p c i k", k=4),
+                in0=xa[:].rearrange("p i (c k) -> p c i k", k=4),
+                in1=xb[:].rearrange("p i (c k) -> p c i k", k=4),
+                op=ALU.min,
+            )
+            codes = held([P, width], U32, f"z_codes{name}")
+            scales = held([P, width], U8, f"z_sc{name}")
+            quantize(codes[:], scales[:], z[:].rearrange("p m i -> p (m i)"))
+            return codes, scales
+
+        xa, xb = picked_tiles(M)
+        for i in range(4):
+            h = features(0, i)
+            pick(h, xa, xb, i, 0, M)
+            if i == 0:
+                deal_w1(1)
+            if i in (1, 2):
+                a = i - 1
+                quantize(w2_codes[a][1][:], w2_sc[a][1][:], round_w2(nc.scalar.copy, a, 1))
+        z0_codes, z0_sc = smaller(xa, xb, M, "0")
+
+        hs = []
+        m0, width = LAST_SLICES[0]
+        xa, xb = picked_tiles(width)
+        for i in range(4):
+            hs.append(features(1, i))
+            pick(hs[i], xa, xb, i, m0, width)
+            if i < 2:
+                quantize(w3_codes[i][:], w3_sc[i][:], round_w3(i))
+
+        out_rows = out.rearrange("(c p) m -> p c m", p=P)
+
+        def second_product(c0, count, m0, width, z1, w_codes, w_sc):
+            bank = psum.tile([P, count, width], F32, name="bank")
+            z_ops = ((z0_codes[:, m0 : m0 + width], z0_sc[:, m0 : m0 + width]), (z1[0][:], z1[1][:]))
+            for c in range(count):
+                cols = slice(P * (c0 + c), P * (c0 + c + 1))
+                for b in range(2):
+                    nc.tensor.matmul_mx(
+                        out=bank[:, c, :],
+                        lhsT=w_codes(b, cols).bitcast(FP8X4),
+                        lhsT_scale=w_sc(b, cols),
+                        rhs=z_ops[b][0].bitcast(FP8X4),
+                        rhs_scale=z_ops[b][1],
+                        start=(b == 0),
+                        stop=(b == 1),
+                    )
+            return bank
+
+        finished = []
+        for k, (m0, width) in enumerate(LAST_SLICES):
+            if k > 0:
+                xa, xb = picked_tiles(width)
+                for i in range(4):
+                    pick(hs[i], xa, xb, i, m0, width)
+            z1 = smaller(xa, xb, width, f"1{k}")
+            count = BANK // width
+            for c0 in range(0, 4, count):
+                y2 = second_product(
+                    c0, count, m0, width, z1, lambda b, cols: w4_codes[:, b, cols], lambda b, cols: w4_sc[4 * b : P, cols]
+                )
+                y1 = second_product(
+                    c0, count, m0, width, z1, lambda b, cols: w3_codes[b][:, cols], lambda b, cols: w3_sc[b][:, cols]
+                )
+                size = work.tile([P, count, width], F32, name="size")
+                damp = work.tile([P, count, width], F32, name="damp", bufs=4)
+                signed = work.tile([P, count, width], F32, name="signed", bufs=4)
+                nc.scalar.activation(out=size[:], in_=y2[:], func=ACT.Abs, bias=zero[:])
+                nc.scalar.activation(out=damp[:], in_=size[:], func=ACT.Exp, bias=zero[:], scale=-1.0)
+                nc.scalar.activation(out=signed[:], in_=y1[:], func=ACT.Tanh, bias=zero[:])
+                finished.append((c0, count, m0, width, signed, damp))
+        for c0, count, m0, width, signed, damp in finished:
+            result = work.tile([P, count, width], F32, name="result", bufs=4)
+            nc.vector.tensor_tensor(out=result[:], in0=signed[:], in1=damp[:], op=ALU.mult)
+            nc.sync.dma_start(out=out_rows[:, c0 : c0 + count, m0 : m0 + width], in_=result[:])

@@ -20,7 +20,6 @@ P = 128
 PASS = 512
 BANK = 512
 LAST_SLICES = ((0, 256), (256, 128), (384, 128))
-GAIN_ON_VECTOR = 8
 
 
 def tile_list_antivenom_panel_features_kernel(
@@ -41,11 +40,11 @@ def tile_list_antivenom_panel_features_kernel(
         tab = [held([P, T], U32, f"tab{a}") for a in range(2)]
         tab_sc = held([P, T], U8, "tab_sc")
         v_sc = [held([P, S], U8, f"v_sc{a}") for a in range(2)]
-        v_words = [[held([P, BANK], U32, f"v_words{a}{half}") for half in range(2)] for a in range(2)]
+        v_words = {(0, half): held([P, BANK], U32, f"v_words{half}") for half in range(2)}
         w1_raw = [held([P, 2, 2 * PASS], U8, f"w1_raw{b}") for b in range(2)]
-        w1_codes = [held([P, 2, 2 * PASS], U8, f"w1_codes{b}") for b in range(2)]
-        w1_sc_raw = held([P, 2, H], U8, "w1_sc_raw")
-        w1_sc = [held([P, 2, PASS], U8, f"w1_sc{b}") for b in range(2)]
+        w1_codes = [held([P, 2, 2 * PASS], U8, "w1_codes0")[:]]
+        w1_sc_raw = held([P, H], U8, "w1_sc_raw")
+        w1_sc = [held([P, H], U8, f"w1_sc{a}") for a in range(2)]
         w2_codes = [[held([P, PASS], U32, f"w2_codes{a}{b}") for b in range(2)] for a in range(2)]
         w2_sc = [[held([P, PASS], U8, f"w2_sc{a}{b}") for b in range(2)] for a in range(2)]
         w3_codes = [held([P, N], U32, f"w3_codes{b}") for b in range(2)]
@@ -53,18 +52,16 @@ def tile_list_antivenom_panel_features_kernel(
         w4_codes = held([P, 2, N], U32, "w4_codes")
         w4_sc = held([P, N], U8, "w4_sc")
         g = held([P, 2, 4], F32, "g")
-        g_neg2 = held([P, 2, 4], F32, "g_neg2")
         wa = held([P, M], F32, "wa")
         wb = held([P, M], F32, "wb")
         zero_in = held([P, 1], F32, "zero_in")
         zero = held([P, 1], F32, "zero")
 
+        nc.vector.memset(tab_sc[:].bitcast(I32), 0)
         nc.vector.memset(zero_in[:], 0.0)
         nc.scalar.activation(out=zero[:], in_=zero_in[:], func=ACT.Silu)
-        nc.vector.memset(tab_sc[:].bitcast(I32), 0)
-        nc.vector.memset(w1_sc_raw[:].bitcast(I32), 0)
-        nc.vector.memset(v_sc[1][:].bitcast(I32), 0)
-        nc.vector.memset(w4_sc[:].bitcast(I32), 0)
+        for plane in (w1_sc_raw, v_sc[1], w1_sc[1], w4_sc):
+            nc.vector.memset(plane[:].bitcast(I32), 0)
 
         def load_rows(w, a, cols):
             raw = work.tile([P, 4, PASS], F32, name="raw", bufs=4)
@@ -85,35 +82,27 @@ def tile_list_antivenom_panel_features_kernel(
                     in_=scales[:, 4 * quad : 4 * quad + 4, :].bitcast(I32),
                 )
 
-        nc.sync.dma_start(list_v[:], offs)
-        w2_raw = {(0, 0): load_rows(w2, 0, slice(0, PASS))}
-        load_packed_scales(tab_sc, tab_scales)
-        for quad in range(4):
-            nc.sync.dma_start(
-                out=w1_sc_raw[32 * quad : 32 * quad + 4, :, :].bitcast(I32),
-                in_=w1_scales[:, 4 * quad : 4 * quad + 4, :].rearrange("a r n -> r a n").bitcast(I32),
-            )
-        w2_raw[1, 0] = load_rows(w2, 1, slice(0, PASS))
-        load_w1(0)
+        def second_pass_plane(planes):
+            nc.gpsimd.dma_start(out=planes[1][0 : P - 4, :].bitcast(I32), in_=planes[0][4:P, :].bitcast(I32))
+
         load_table(0)
+        nc.sync.dma_start(list_v[:], offs)
+        load_packed_scales(tab_sc, tab_scales)
         load_table(1)
+        load_w1(0)
+        load_packed_scales(w1_sc_raw, w1_scales)
+        w2_raw = {(a, 0): load_rows(w2, a, slice(0, PASS)) for a in range(2)}
         nc.sync.dma_start(out=g[:], in_=gain.rearrange("(b p i) -> p b i", b=2, i=4))
+        w2_raw[0, 1] = load_rows(w2, 0, slice(PASS, 2 * PASS))
         nc.sync.dma_start(list_a[:], offs2)
         nc.sync.dma_start(list_b[:], offs3)
         nc.sync.dma_start(out=wa[:], in_=wga)
         nc.sync.dma_start(out=wb[:], in_=wgb)
+        w2_raw[1, 1] = load_rows(w2, 1, slice(PASS, 2 * PASS))
         load_w1(1)
-        for a in range(2):
-            w2_raw[a, 1] = load_rows(w2, a, slice(PASS, 2 * PASS))
         w3_raw = [load_rows(w3, b, slice(0, N)) for b in range(2)]
         nc.sync.dma_start(out=w4_codes[:].bitcast(I32), in_=w4_words.rearrange("a p c i -> p a (c i)").bitcast(I32))
         load_packed_scales(w4_sc, w4_scales)
-
-        def deal_w1_scales(b):
-            nc.vector.tensor_copy(
-                out=w1_sc[b][:].rearrange("p a (t q) -> p a t q", t=4),
-                in_=w1_sc_raw[:, :, PASS * b : PASS * (b + 1)].rearrange("p a (q t) -> p a t q", t=4),
-            )
 
         def deal_w1(b):
             nc.scalar.copy(
@@ -123,18 +112,17 @@ def tile_list_antivenom_panel_features_kernel(
 
         def gather_words(a, half):
             cols = slice(half * BANK // 16, (half + 1) * BANK // 16)
-            nc.vector.tensor_copy(out=v_words[a][half][:], in_=tab[a][:].indirect(list_v[:, cols]))
+            nc.vector.tensor_copy(out=v_words[a, half][:], in_=tab[a][:].indirect(list_v[:, cols]))
 
-        def round_w2(copy, a, b):
-            grouped = work.tile([P, 4, P, 4], BF16, name="grouped", align_bytes=64)
+        def round_w2(copy, a, b, grouped):
             copy(
                 out=grouped[:].rearrange("p t q j -> p q j t"),
                 in_=w2_raw[a, b][:].rearrange("p j (q t) -> p q j t", t=4),
             )
             return grouped[:].rearrange("p t q j -> p (t q j)")
 
-        def round_w3(b):
-            grouped = work.tile([P, N, 4], BF16, name="grouped", align_bytes=64)
+        def round_w3(b, spent):
+            grouped = spent[:].bitcast(BF16).rearrange("p (c j) -> p c j", j=4)
             nc.scalar.copy(
                 out=grouped[:].rearrange("p (c k) j -> p c j k", k=4),
                 in_=w3_raw[b][:].rearrange("p j (c k) -> p c j k", k=4),
@@ -144,19 +132,29 @@ def tile_list_antivenom_panel_features_kernel(
         def quantize(codes, scales, values):
             nc.vector.quantize_mx(out=codes.bitcast(FP8X4), scales=scales, in_=values)
 
-        rounded = [round_w2(nc.scalar.copy, a, 0) for a in range(2)]
+        def staged():
+            return work.tile([P, 4, P, 4], BF16, name="grouped", align_bytes=64)
+
         deal_w1(0)
-        nc.vector.tensor_copy(out=v_sc[0][:], in_=tab_sc[:].indirect(list_v[:]))
-        nc.gpsimd.dma_start(out=v_sc[1][0 : P - 4, :].bitcast(I32), in_=v_sc[0][4:P, :].bitcast(I32))
-        for b in range(2):
-            deal_w1_scales(b)
-        quantize(w2_codes[0][0][:], w2_sc[0][0][:], rounded[0])
+        rounded = round_w2(nc.scalar.copy, 0, 0, staged())
         gather_words(0, 0)
         gather_words(0, 1)
-        quantize(w2_codes[1][0][:], w2_sc[1][0][:], rounded[1])
+        nc.vector.tensor_copy(out=v_sc[0][:], in_=tab_sc[:].indirect(list_v[:]))
+        second_pass_plane(v_sc)
+        nc.vector.tensor_copy(
+            out=w1_sc[0][:].rearrange("p (b t q) -> p b t q", b=2, t=4),
+            in_=w1_sc_raw[:].rearrange("p (b q t) -> p b t q", b=2, t=4),
+        )
+        second_pass_plane(w1_sc)
+        v_words[1, 0] = held([P, BANK], U32, "tab_sc")
+        v_words[1, 1] = held([P, BANK], U32, "w1_sc_raw")
         gather_words(1, 0)
         gather_words(1, 1)
-        nc.vector.tensor_scalar(out=g_neg2[:], in0=g[:], scalar1=-2.0, scalar2=None, op0=ALU.mult)
+        rounded = [rounded, round_w2(nc.vector.tensor_copy, 1, 0, staged())]
+        for c0, c1 in ((0, P), (P, PASS)):
+            for a in range(2):
+                quantize(w2_codes[a][0][:, c0:c1], w2_sc[a][0][:, c0:c1], rounded[a][:, 4 * c0 : 4 * c1])
+        quantize(w2_codes[0][1][:], w2_sc[0][1][:], round_w2(nc.vector.tensor_copy, 0, 1, staged()))
 
         def first_product(half, stationary):
             bank = psum.tile([P, BANK], F32, name="bank")
@@ -167,7 +165,7 @@ def tile_list_antivenom_panel_features_kernel(
                     out=bank[:],
                     lhsT=codes,
                     lhsT_scale=scales,
-                    rhs=v_words[a][half][:].bitcast(FP8X4),
+                    rhs=v_words[a, half][:].bitcast(FP8X4),
                     rhs_scale=v_sc[a][:, cols],
                     start=(a == 0),
                     stop=(a == 1),
@@ -175,36 +173,31 @@ def tile_list_antivenom_panel_features_kernel(
             return bank
 
         def features(b, i):
-            th = work.tile([P, S], F32, name="th", bufs=3)
-            sn = work.tile([P, S], F32, name="sn")
+            if b == 0:
+                th = w2_raw[i // 2, 0][:].rearrange("p (u j) c -> p u (j c)", u=2)[:, i % 2, :]
+            else:
+                th = work.tile([P, S], F32, name="th", bufs=3)
+            sn = work.tile([P, S], F32, name="sn", align_bytes=64)
             rows = slice(P * i, P * (i + 1))
             for half in range(2):
                 cols = slice(half * BANK, (half + 1) * BANK)
                 a1 = first_product(
                     half,
-                    lambda a: (w1_codes[b][:, a, 2 * P * i : 2 * P * (i + 1)].bitcast(FP4X4), w1_sc[b][:, a, rows]),
+                    lambda a: (w1_codes[b][:, a, 2 * P * i : 2 * P * (i + 1)].bitcast(FP4X4), w1_sc[a][:, PASS * b + P * i : PASS * b + P * (i + 1)]),
                 )
                 nc.scalar.activation(out=th[:, cols], in_=a1[:], func=ACT.Tanh, bias=zero[:])
             for half in range(2):
                 cols = slice(half * BANK, (half + 1) * BANK)
                 a2 = first_product(half, lambda a: (w2_codes[a][b][:, rows].bitcast(FP8X4), w2_sc[a][b][:, rows]))
                 nc.scalar.activation(out=sn[:, cols], in_=a2[:], func=ACT.Sin, bias=zero[:], scale=0.5)
-            sq = work.tile([P, S], F32, name="sq", bufs=2)
+            sq = held([P, S], F32, "first_sq") if (b, i) == (0, 0) else work.tile([P, S], F32, name="sq", bufs=3, align_bytes=64)
             nc.scalar.activation(out=sq[:], in_=sn[:], func=ACT.Square, bias=zero[:])
             gi = g[:, b, i : i + 1]
             h = work.tile([P, S], F32, name="h", bufs=5)
-            part = work.tile([P, S], F32, name="part", bufs=3)
-            if 4 * b + i < GAIN_ON_VECTOR:
-                nc.vector.scalar_tensor_tensor(
-                    out=part[:], in0=sq[:], scalar=-2.0, in1=th[:], op0=ALU.mult, op1=ALU.add
-                )
-                nc.vector.tensor_scalar(out=h[:], in0=part[:], scalar1=1.0, scalar2=gi, op0=ALU.add, op1=ALU.mult)
-            else:
-                nc.scalar.activation(
-                    out=part[:], in_=sq[:], func=ACT.Identity, bias=gi, scale=g_neg2[:, b, i : i + 1]
-                )
-                nc.vector.scalar_tensor_tensor(out=h[:], in0=th[:], scalar=gi, in1=part[:], op0=ALU.mult, op1=ALU.add)
-            return h
+            part = work.tile([P, S], F32, name="part")
+            nc.vector.scalar_tensor_tensor(out=part[:], in0=sq[:], scalar=-2.0, in1=th[:], op0=ALU.mult, op1=ALU.add)
+            nc.vector.tensor_scalar(out=h[:], in0=part[:], scalar1=1.0, scalar2=gi, op0=ALU.add, op1=ALU.mult)
+            return h, sn, sq
 
         def picked_tiles(width):
             xa = work.tile([P, 4, width], F32, name="xa", bufs=1)
@@ -231,25 +224,30 @@ def tile_list_antivenom_panel_features_kernel(
             quantize(codes[:], scales[:], z[:].rearrange("p m i -> p (m i)"))
             return codes, scales
 
+        squares = []
         xa, xb = picked_tiles(M)
         for i in range(4):
-            h = features(0, i)
+            h, sn, sq = features(0, i)
+            squares.append(sq)
             pick(h, xa, xb, i, 0, M)
-            if i == 0:
+            if i == 1:
+                w1_codes.append(held([P, 2, 2 * PASS], U8, "first_sq")[:])
                 deal_w1(1)
-            if i in (1, 2):
-                a = i - 1
-                quantize(w2_codes[a][1][:], w2_sc[a][1][:], round_w2(nc.scalar.copy, a, 1))
+            if i == 2:
+                grouped = squares[1][:].bitcast(BF16).rearrange("p (t q j) -> p t q j", t=4, j=4)
+                quantize(w2_codes[1][1][:], w2_sc[1][1][:], round_w2(nc.scalar.copy, 1, 1, grouped))
         z0_codes, z0_sc = smaller(xa, xb, M, "0")
 
         hs = []
+        sines = []
         m0, width = LAST_SLICES[0]
         xa, xb = picked_tiles(width)
         for i in range(4):
-            hs.append(features(1, i))
+            h, sn, sq = features(1, i)
+            hs.append(h)
+            sines.append(sn)
             pick(hs[i], xa, xb, i, m0, width)
-            if i < 2:
-                quantize(w3_codes[i][:], w3_sc[i][:], round_w3(i))
+        w3_rounded = [round_w3(b, sines[2 + b]) for b in range(2)]
 
         out_rows = out.rearrange("(c p) m -> p c m", p=P)
 
@@ -277,6 +275,9 @@ def tile_list_antivenom_panel_features_kernel(
                 for i in range(4):
                     pick(hs[i], xa, xb, i, m0, width)
             z1 = smaller(xa, xb, width, f"1{k}")
+            if k == 0:
+                for b in range(2):
+                    quantize(w3_codes[b][:], w3_sc[b][:], w3_rounded[b])
             count = BANK // width
             for c0 in range(0, 4, count):
                 y2 = second_product(

@@ -40,31 +40,28 @@ def tile_list_antivenom_panel_features_kernel(
         tab = [held([P, T], U32, f"tab{a}") for a in range(2)]
         tab_sc = held([P, T], U8, "tab_sc")
         v_sc = [held([P, S], U8, f"v_sc{a}") for a in range(2)]
-        v_words = {(0, half): held([P, BANK], U32, f"v_words{half}") for half in range(2)}
-        w1_raw = [held([P, 2, 2 * PASS], U8, f"w1_raw{b}") for b in range(2)]
+        v_words = {(0, 0): held([P, BANK], U32, "v_words_first")[:]}
+        w1_raw = [held([P, 2, 2 * PASS], U8, "w1_raw0")]
         w1_codes = [held([P, 2, 2 * PASS], U8, "w1_codes0")[:]]
         w1_sc_raw = held([P, H], U8, "w1_sc_raw")
-        w1_sc = [held([P, H], U8, f"w1_sc{a}") for a in range(2)]
+        w1_sc = {1: held([P, H], U8, "w1_sc1")}
         w2_codes = [[held([P, PASS], U32, f"w2_codes{a}{b}") for b in range(2)] for a in range(2)]
         w2_sc = [[held([P, PASS], U8, f"w2_sc{a}{b}") for b in range(2)] for a in range(2)]
         w3_codes = [held([P, N], U32, f"w3_codes{b}") for b in range(2)]
         w3_sc = [held([P, N], U8, f"w3_sc{b}") for b in range(2)]
-        w4_codes = held([P, 2, N], U32, "w4_codes")
         w4_sc = held([P, N], U8, "w4_sc")
         g = held([P, 2, 4], F32, "g")
-        wa = held([P, M], F32, "wa")
-        wb = held([P, M], F32, "wb")
         zero_in = held([P, 1], F32, "zero_in")
         zero = held([P, 1], F32, "zero")
 
         nc.vector.memset(tab_sc[:].bitcast(I32), 0)
         nc.vector.memset(zero_in[:], 0.0)
         nc.scalar.activation(out=zero[:], in_=zero_in[:], func=ACT.Silu)
-        for plane in (w1_sc_raw, v_sc[1], w1_sc[1], w4_sc):
+        for plane in (w1_sc_raw, v_sc[1], w1_sc[1]):
             nc.vector.memset(plane[:].bitcast(I32), 0)
+        nc.gpsimd.memset(w4_sc[:].bitcast(I32), 0)
 
-        def load_rows(w, a, cols):
-            raw = work.tile([P, 4, PASS], F32, name="raw", bufs=4)
+        def load_rows(w, a, cols, raw):
             nc.sync.dma_start(out=raw[:], in_=w[PASS * a : PASS * (a + 1), cols].rearrange("(p j) c -> p j c", j=4))
             return raw
 
@@ -83,7 +80,7 @@ def tile_list_antivenom_panel_features_kernel(
                 )
 
         def second_pass_plane(planes):
-            nc.gpsimd.dma_start(out=planes[1][0 : P - 4, :].bitcast(I32), in_=planes[0][4:P, :].bitcast(I32))
+            nc.sync.dma_start(out=planes[1][0:112, :].bitcast(I32), in_=planes[0][4:116, :].bitcast(I32))
 
         load_table(0)
         nc.sync.dma_start(list_v[:], offs)
@@ -91,18 +88,10 @@ def tile_list_antivenom_panel_features_kernel(
         load_table(1)
         load_w1(0)
         load_packed_scales(w1_sc_raw, w1_scales)
-        w2_raw = {(a, 0): load_rows(w2, a, slice(0, PASS)) for a in range(2)}
+        w2_raw = {(a, 0): load_rows(w2, a, slice(0, PASS), held([P, 4, PASS], F32, f"w2_first{a}")) for a in range(2)}
         nc.sync.dma_start(out=g[:], in_=gain.rearrange("(b p i) -> p b i", b=2, i=4))
-        w2_raw[0, 1] = load_rows(w2, 0, slice(PASS, 2 * PASS))
         nc.sync.dma_start(list_a[:], offs2)
         nc.sync.dma_start(list_b[:], offs3)
-        nc.sync.dma_start(out=wa[:], in_=wga)
-        nc.sync.dma_start(out=wb[:], in_=wgb)
-        w2_raw[1, 1] = load_rows(w2, 1, slice(PASS, 2 * PASS))
-        load_w1(1)
-        w3_raw = [load_rows(w3, b, slice(0, N)) for b in range(2)]
-        nc.sync.dma_start(out=w4_codes[:].bitcast(I32), in_=w4_words.rearrange("a p c i -> p a (c i)").bitcast(I32))
-        load_packed_scales(w4_sc, w4_scales)
 
         def deal_w1(b):
             nc.scalar.copy(
@@ -132,29 +121,41 @@ def tile_list_antivenom_panel_features_kernel(
         def quantize(codes, scales, values):
             nc.vector.quantize_mx(out=codes.bitcast(FP8X4), scales=scales, in_=values)
 
-        def staged():
-            return work.tile([P, 4, P, 4], BF16, name="grouped", align_bytes=64)
+        def staged(k):
+            return held([P, 4, P, 4], BF16, f"staged{k}")
 
         deal_w1(0)
-        rounded = round_w2(nc.scalar.copy, 0, 0, staged())
+        rounded = round_w2(nc.scalar.copy, 0, 0, staged(0))
         gather_words(0, 0)
-        gather_words(0, 1)
         nc.vector.tensor_copy(out=v_sc[0][:], in_=tab_sc[:].indirect(list_v[:]))
         second_pass_plane(v_sc)
+        w1_sc[0] = held([P, H], U8, "tab_sc")
         nc.vector.tensor_copy(
             out=w1_sc[0][:].rearrange("p (b t q) -> p b t q", b=2, t=4),
             in_=w1_sc_raw[:].rearrange("p (b q t) -> p b t q", b=2, t=4),
         )
         second_pass_plane(w1_sc)
-        v_words[1, 0] = held([P, BANK], U32, "tab_sc")
-        v_words[1, 1] = held([P, BANK], U32, "w1_sc_raw")
-        gather_words(1, 0)
-        gather_words(1, 1)
-        rounded = [rounded, round_w2(nc.vector.tensor_copy, 1, 0, staged())]
+        later_words = held([P, 3, BANK], U32, "w1_sc_raw")
+        for k, (a, half) in enumerate(((0, 1), (1, 0), (1, 1))):
+            v_words[a, half] = later_words[:, k, :]
+            gather_words(a, half)
+        w2_raw[0, 1] = load_rows(w2, 0, slice(PASS, 2 * PASS), held([P, 4, PASS], F32, "tab0"))
+        weights = held([P, 2, M], F32, "tab1")
+        wa, wb = weights[:, 0, :], weights[:, 1, :]
+        nc.sync.dma_start(out=wa, in_=wga)
+        nc.sync.dma_start(out=wb, in_=wgb)
+        rounded = [rounded, round_w2(nc.vector.tensor_copy, 1, 0, staged(1))]
         for c0, c1 in ((0, P), (P, PASS)):
             for a in range(2):
                 quantize(w2_codes[a][0][:, c0:c1], w2_sc[a][0][:, c0:c1], rounded[a][:, 4 * c0 : 4 * c1])
-        quantize(w2_codes[0][1][:], w2_sc[0][1][:], round_w2(nc.vector.tensor_copy, 0, 1, staged()))
+        quantize(w2_codes[0][1][:], w2_sc[0][1][:], round_w2(nc.vector.tensor_copy, 0, 1, staged(2)))
+        w1_raw.append(held([P, 2, 2 * PASS], U8, "staged1"))
+        load_w1(1)
+        w2_raw[1, 1] = load_rows(w2, 1, slice(PASS, 2 * PASS), held([P, 4, PASS], F32, "staged0"))
+        w3_raw = [load_rows(w3, 0, slice(0, N), held([P, 4, N], F32, "tab0"))]
+        w4_codes = held([P, 2, N], U32, "staged2")
+        nc.sync.dma_start(out=w4_codes[:].bitcast(I32), in_=w4_words.rearrange("a p c i -> p a (c i)").bitcast(I32))
+        load_packed_scales(w4_sc, w4_scales)
 
         def first_product(half, stationary):
             bank = psum.tile([P, BANK], F32, name="bank")
@@ -236,6 +237,7 @@ def tile_list_antivenom_panel_features_kernel(
             if i == 2:
                 grouped = squares[1][:].bitcast(BF16).rearrange("p (t q j) -> p t q j", t=4, j=4)
                 quantize(w2_codes[1][1][:], w2_sc[1][1][:], round_w2(nc.scalar.copy, 1, 1, grouped))
+                w3_raw.append(load_rows(w3, 1, slice(0, N), held([P, 4, N], F32, "staged0")))
         z0_codes, z0_sc = smaller(xa, xb, M, "0")
 
         hs = []

@@ -19,7 +19,8 @@ ACT = mybir.ActivationFunctionType
 P = 128
 PASS = 512
 BANK = 512
-LAST_SLICES = ((0, 256), (256, 128), (384, 128))
+LAST_SLICES = ((0, 128), (128, 256), (384, 128))
+GAIN_ON_VECTOR = 3
 
 
 def tile_list_antivenom_panel_features_kernel(
@@ -51,6 +52,7 @@ def tile_list_antivenom_panel_features_kernel(
         w3_sc = [held([P, N], U8, f"w3_sc{b}") for b in range(2)]
         w4_sc = held([P, N], U8, "w4_sc")
         g = held([P, 2, 4], F32, "g")
+        g_neg2 = held([P, 2, 4], F32, "g_neg2")
         zero_in = held([P, 1], F32, "zero_in")
         zero = held([P, 1], F32, "zero")
 
@@ -149,6 +151,7 @@ def tile_list_antivenom_panel_features_kernel(
             for a in range(2):
                 quantize(w2_codes[a][0][:, c0:c1], w2_sc[a][0][:, c0:c1], rounded[a][:, 4 * c0 : 4 * c1])
         quantize(w2_codes[0][1][:], w2_sc[0][1][:], round_w2(nc.vector.tensor_copy, 0, 1, staged(2)))
+        nc.vector.tensor_scalar(out=g_neg2[:], in0=g[:], scalar1=-2.0, scalar2=None, op0=ALU.mult)
         w1_raw.append(held([P, 2, 2 * PASS], U8, "staged1"))
         load_w1(1)
         w2_raw[1, 1] = load_rows(w2, 1, slice(PASS, 2 * PASS), held([P, 4, PASS], F32, "staged0"))
@@ -194,10 +197,18 @@ def tile_list_antivenom_panel_features_kernel(
             sq = held([P, S], F32, "first_sq") if (b, i) == (0, 0) else work.tile([P, S], F32, name="sq", bufs=3, align_bytes=64)
             nc.scalar.activation(out=sq[:], in_=sn[:], func=ACT.Square, bias=zero[:])
             gi = g[:, b, i : i + 1]
-            h = work.tile([P, S], F32, name="h", bufs=5)
-            part = work.tile([P, S], F32, name="part")
-            nc.vector.scalar_tensor_tensor(out=part[:], in0=sq[:], scalar=-2.0, in1=th[:], op0=ALU.mult, op1=ALU.add)
-            nc.vector.tensor_scalar(out=h[:], in0=part[:], scalar1=1.0, scalar2=gi, op0=ALU.add, op1=ALU.mult)
+            h = work.tile([P, S], F32, name="h", bufs=2)
+            part = work.tile([P, S], F32, name="part", bufs=3)
+            if 4 * b + i < GAIN_ON_VECTOR:
+                nc.vector.scalar_tensor_tensor(
+                    out=part[:], in0=sq[:], scalar=-2.0, in1=th[:], op0=ALU.mult, op1=ALU.add
+                )
+                nc.vector.tensor_scalar(out=h[:], in0=part[:], scalar1=1.0, scalar2=gi, op0=ALU.add, op1=ALU.mult)
+            else:
+                nc.scalar.activation(
+                    out=part[:], in_=sq[:], func=ACT.Identity, bias=gi, scale=g_neg2[:, b, i : i + 1]
+                )
+                nc.vector.scalar_tensor_tensor(out=h[:], in0=th[:], scalar=gi, in1=part[:], op0=ALU.mult, op1=ALU.add)
             return h, sn, sq
 
         def picked_tiles(width):
@@ -209,15 +220,15 @@ def tile_list_antivenom_panel_features_kernel(
             cols = slice(m0 // 16, (m0 + width) // 16)
             for x, offsets, weight in ((xa, list_a, wa), (xb, list_b, wb)):
                 nc.vector.tensor_tensor(
-                    out=x[:, i, :], in0=h[:].indirect(offsets[:, cols]), in1=weight[:, m0 : m0 + width], op=ALU.mult
+                    out=x[:, i, m0 : m0 + width], in0=h[:].indirect(offsets[:, cols]), in1=weight[:, m0 : m0 + width], op=ALU.mult
                 )
 
-        def smaller(xa, xb, width, name):
+        def smaller(xa, xb, m0, width, name):
             z = keep.tile([P, width, 4], BF16, name=f"z{name}", align_bytes=64)
             nc.vector.tensor_tensor(
                 out=z[:].rearrange("p (c k) i -> p c i k", k=4),
-                in0=xa[:].rearrange("p i (c k) -> p c i k", k=4),
-                in1=xb[:].rearrange("p i (c k) -> p c i k", k=4),
+                in0=xa[:, :, m0 : m0 + width].rearrange("p i (c k) -> p c i k", k=4),
+                in1=xb[:, :, m0 : m0 + width].rearrange("p i (c k) -> p c i k", k=4),
                 op=ALU.min,
             )
             codes = held([P, width], U32, f"z_codes{name}")
@@ -238,17 +249,15 @@ def tile_list_antivenom_panel_features_kernel(
                 grouped = squares[1][:].bitcast(BF16).rearrange("p (t q j) -> p t q j", t=4, j=4)
                 quantize(w2_codes[1][1][:], w2_sc[1][1][:], round_w2(nc.scalar.copy, 1, 1, grouped))
                 w3_raw.append(load_rows(w3, 1, slice(0, N), held([P, 4, N], F32, "staged0")))
-        z0_codes, z0_sc = smaller(xa, xb, M, "0")
+        z0_codes, z0_sc = smaller(xa, xb, 0, M, "0")
 
-        hs = []
         sines = []
-        m0, width = LAST_SLICES[0]
-        xa, xb = picked_tiles(width)
+        xa, xb = picked_tiles(M)
         for i in range(4):
             h, sn, sq = features(1, i)
-            hs.append(h)
             sines.append(sn)
-            pick(hs[i], xa, xb, i, m0, width)
+            if i < 3:
+                pick(h, xa, xb, i, 0, M)
         w3_rounded = [round_w3(b, sines[2 + b]) for b in range(2)]
 
         out_rows = out.rearrange("(c p) m -> p c m", p=P)
@@ -272,11 +281,8 @@ def tile_list_antivenom_panel_features_kernel(
 
         finished = []
         for k, (m0, width) in enumerate(LAST_SLICES):
-            if k > 0:
-                xa, xb = picked_tiles(width)
-                for i in range(4):
-                    pick(hs[i], xa, xb, i, m0, width)
-            z1 = smaller(xa, xb, width, f"1{k}")
+            pick(h, xa, xb, 3, m0, width)
+            z1 = smaller(xa, xb, m0, width, f"1{k}")
             if k == 0:
                 for b in range(2):
                     quantize(w3_codes[b][:], w3_sc[b][:], w3_rounded[b])

@@ -19,8 +19,7 @@ ACT = mybir.ActivationFunctionType
 P = 128
 PASS = 512
 BANK = 512
-LAST_SLICES = ((0, 128), (128, 256), (384, 128))
-GAIN_ON_VECTOR = 3
+OUT_SLICES = ((0, 128), (128, 256), (384, 128))
 
 
 def tile_list_antivenom_panel_features_kernel(
@@ -32,36 +31,36 @@ def tile_list_antivenom_panel_features_kernel(
         work = ctx.enter_context(tc.tile_pool(name="work", bufs=2))
         psum = ctx.enter_context(tc.psum_pool(name="psum", bufs=8))
 
-        def held(shape, dtype, name):
-            return keep.tile(shape, dtype, name=name, align_bytes=64)
+        def held(shape, dtype, tag):
+            return keep.tile(shape, dtype, name=tag, align_bytes=64)
 
         list_v = keep.tile([P, S // 16], U16, name="list_v")
         list_a = keep.tile([P, M // 16], U16, name="list_a")
         list_b = keep.tile([P, M // 16], U16, name="list_b")
         tab = [held([P, T], U32, f"tab{a}") for a in range(2)]
         tab_sc = held([P, T], U8, "tab_sc")
-        v_sc = [held([P, S], U8, f"v_sc{a}") for a in range(2)]
-        v_words = {(0, 0): held([P, BANK], U32, "v_words_first")[:]}
+        picked_sc = held([P, S], U8, "picked_sc")
+        v_sc = held([P, 2, S], U8, "v_sc")
+        v_words = {}
         w1_raw = [held([P, 2, 2 * PASS], U8, "w1_raw0")]
-        w1_codes = [held([P, 2, 2 * PASS], U8, "w1_codes0")[:]]
-        w1_sc_raw = held([P, H], U8, "w1_sc_raw")
-        w1_sc = {1: held([P, H], U8, "w1_sc1")}
+        w1_codes = [held([P, 2, 2 * PASS], U8, "w1_codes0")]
+        w1_sc_raw = held([P, 2, H], U8, "w1_sc_raw")
+        w1_sc = held([P, 2, H], U8, "w1_sc")
         w2_codes = [[held([P, PASS], U32, f"w2_codes{a}{b}") for b in range(2)] for a in range(2)]
         w2_sc = [[held([P, PASS], U8, f"w2_sc{a}{b}") for b in range(2)] for a in range(2)]
         w3_codes = [held([P, N], U32, f"w3_codes{b}") for b in range(2)]
         w3_sc = [held([P, N], U8, f"w3_sc{b}") for b in range(2)]
-        w4_sc = held([P, N], U8, "w4_sc")
         g = held([P, 2, 4], F32, "g")
-        g_neg2 = held([P, 2, 4], F32, "g_neg2")
+        g_neg2 = held([P, 4], F32, "g_neg2")
         zero_in = held([P, 1], F32, "zero_in")
         zero = held([P, 1], F32, "zero")
 
-        nc.vector.memset(tab_sc[:].bitcast(I32), 0)
+        nc.vector.memset(w1_sc_raw[:].bitcast(I32), 0)
         nc.vector.memset(zero_in[:], 0.0)
         nc.scalar.activation(out=zero[:], in_=zero_in[:], func=ACT.Silu)
-        for plane in (w1_sc_raw, v_sc[1], w1_sc[1]):
-            nc.vector.memset(plane[:].bitcast(I32), 0)
-        nc.gpsimd.memset(w4_sc[:].bitcast(I32), 0)
+        for rows in (slice(32, 64), slice(64, P)):
+            nc.vector.memset(tab_sc[rows, :].bitcast(I32), 0)
+        nc.vector.memset(v_sc[:].bitcast(I32), 0)
 
         def load_rows(w, a, cols, raw):
             nc.sync.dma_start(out=raw[:], in_=w[PASS * a : PASS * (a + 1), cols].rearrange("(p j) c -> p j c", j=4))
@@ -74,22 +73,16 @@ def tile_list_antivenom_panel_features_kernel(
         def load_table(a):
             nc.sync.dma_start(out=tab[a][:].bitcast(I32), in_=tab_words[a].rearrange("p t i -> p (t i)").bitcast(I32))
 
-        def load_packed_scales(plane, scales):
-            for quad in range(4):
-                nc.sync.dma_start(
-                    out=plane[32 * quad : 32 * quad + 8, :].bitcast(I32),
-                    in_=scales[:, 4 * quad : 4 * quad + 4, :].bitcast(I32),
-                )
-
-        def second_pass_plane(planes):
-            nc.sync.dma_start(out=planes[1][0:112, :].bitcast(I32), in_=planes[0][4:116, :].bitcast(I32))
-
-        load_table(0)
+        nc.sync.dma_start(out=tab_sc[0:32, :].bitcast(I32), in_=tab_scales.rearrange("a q t -> q a t").bitcast(I32))
         nc.sync.dma_start(list_v[:], offs)
-        load_packed_scales(tab_sc, tab_scales)
+        load_table(0)
+        for quad in range(4):
+            nc.sync.dma_start(
+                out=w1_sc_raw[32 * quad : 32 * quad + 4, :, :].bitcast(I32),
+                in_=w1_scales[:, 4 * quad : 4 * quad + 4, :].rearrange("a s n -> s a n").bitcast(I32),
+            )
         load_table(1)
         load_w1(0)
-        load_packed_scales(w1_sc_raw, w1_scales)
         w2_raw = {(a, 0): load_rows(w2, a, slice(0, PASS), held([P, 4, PASS], F32, f"w2_first{a}")) for a in range(2)}
         nc.sync.dma_start(out=g[:], in_=gain.rearrange("(b p i) -> p b i", b=2, i=4))
         nc.sync.dma_start(list_a[:], offs2)
@@ -103,7 +96,7 @@ def tile_list_antivenom_panel_features_kernel(
 
         def gather_words(a, half):
             cols = slice(half * BANK // 16, (half + 1) * BANK // 16)
-            nc.vector.tensor_copy(out=v_words[a, half][:], in_=tab[a][:].indirect(list_v[:, cols]))
+            nc.vector.tensor_copy(out=v_words[a, half], in_=tab[a][:].indirect(list_v[:, cols]))
 
         def round_w2(copy, a, b, grouped):
             copy(
@@ -115,62 +108,73 @@ def tile_list_antivenom_panel_features_kernel(
         def round_w3(b, spent):
             grouped = spent[:].bitcast(BF16).rearrange("p (c j) -> p c j", j=4)
             nc.scalar.copy(
-                out=grouped[:].rearrange("p (c k) j -> p c j k", k=4),
-                in_=w3_raw[b][:].rearrange("p j (c k) -> p c j k", k=4),
+                out=grouped[:].rearrange("p (c u) j -> p c j u", u=4),
+                in_=w3_raw[b][:].rearrange("p j (c u) -> p c j u", u=4),
             )
             return grouped[:].rearrange("p c j -> p (c j)")
 
         def quantize(codes, scales, values):
             nc.vector.quantize_mx(out=codes.bitcast(FP8X4), scales=scales, in_=values)
 
-        def staged(k):
-            return held([P, 4, P, 4], BF16, f"staged{k}")
+        def staged(number):
+            return held([P, 4, P, 4], BF16, f"staged{number}")
 
         deal_w1(0)
-        rounded = round_w2(nc.scalar.copy, 0, 0, staged(0))
-        gather_words(0, 0)
-        nc.vector.tensor_copy(out=v_sc[0][:], in_=tab_sc[:].indirect(list_v[:]))
-        second_pass_plane(v_sc)
-        w1_sc[0] = held([P, H], U8, "tab_sc")
+        w2_rounded = [round_w2(nc.scalar.copy, 0, 0, staged(0))]
+        nc.vector.tensor_copy(out=picked_sc[:], in_=tab_sc[:].indirect(list_v[:]))
+        for quad in range(4):
+            nc.sync.dma_start(
+                out=v_sc[32 * quad : 32 * quad + 4, :, :].bitcast(I32),
+                in_=picked_sc[8 * quad : 8 * quad + 8, :].bitcast(I32),
+            )
+        first_words = held([P, 2, BANK], U32, "tab_sc")
+        for half in range(2):
+            v_words[0, half] = first_words[:, half, :]
+            gather_words(0, half)
         nc.vector.tensor_copy(
-            out=w1_sc[0][:].rearrange("p (b t q) -> p b t q", b=2, t=4),
-            in_=w1_sc_raw[:].rearrange("p (b q t) -> p b t q", b=2, t=4),
+            out=w1_sc[:].rearrange("p a (b t q) -> p (a b) t q", b=2, t=4),
+            in_=w1_sc_raw[:].rearrange("p a (b q t) -> p (a b) t q", b=2, t=4),
         )
-        second_pass_plane(w1_sc)
-        later_words = held([P, 3, BANK], U32, "w1_sc_raw")
-        for k, (a, half) in enumerate(((0, 1), (1, 0), (1, 1))):
-            v_words[a, half] = later_words[:, k, :]
-            gather_words(a, half)
+        second_words = held([P, 2, BANK], U32, "w1_sc_raw")
+        for half in range(2):
+            v_words[1, half] = second_words[:, half, :]
+            gather_words(1, half)
+
         w2_raw[0, 1] = load_rows(w2, 0, slice(PASS, 2 * PASS), held([P, 4, PASS], F32, "tab0"))
         weights = held([P, 2, M], F32, "tab1")
         wa, wb = weights[:, 0, :], weights[:, 1, :]
         nc.sync.dma_start(out=wa, in_=wga)
         nc.sync.dma_start(out=wb, in_=wgb)
-        rounded = [rounded, round_w2(nc.vector.tensor_copy, 1, 0, staged(1))]
+        w2_rounded.append(round_w2(nc.vector.tensor_copy, 1, 0, staged(1)))
         for c0, c1 in ((0, P), (P, PASS)):
             for a in range(2):
-                quantize(w2_codes[a][0][:, c0:c1], w2_sc[a][0][:, c0:c1], rounded[a][:, 4 * c0 : 4 * c1])
+                quantize(w2_codes[a][0][:, c0:c1], w2_sc[a][0][:, c0:c1], w2_rounded[a][:, 4 * c0 : 4 * c1])
         quantize(w2_codes[0][1][:], w2_sc[0][1][:], round_w2(nc.vector.tensor_copy, 0, 1, staged(2)))
-        nc.vector.tensor_scalar(out=g_neg2[:], in0=g[:], scalar1=-2.0, scalar2=None, op0=ALU.mult)
+        nc.vector.tensor_scalar(out=g_neg2[:], in0=g[:, 1, :], scalar1=-2.0, scalar2=None, op0=ALU.mult)
         w1_raw.append(held([P, 2, 2 * PASS], U8, "staged1"))
         load_w1(1)
         w2_raw[1, 1] = load_rows(w2, 1, slice(PASS, 2 * PASS), held([P, 4, PASS], F32, "staged0"))
         w3_raw = [load_rows(w3, 0, slice(0, N), held([P, 4, N], F32, "tab0"))]
         w4_codes = held([P, 2, N], U32, "staged2")
         nc.sync.dma_start(out=w4_codes[:].bitcast(I32), in_=w4_words.rearrange("a p c i -> p a (c i)").bitcast(I32))
-        load_packed_scales(w4_sc, w4_scales)
+        w4_sc = held([P, N], U8, "picked_sc")
+        nc.gpsimd.memset(w4_sc[:].bitcast(I32), 0)
+        for quad in range(4):
+            nc.sync.dma_start(
+                out=w4_sc[32 * quad : 32 * quad + 8, :].bitcast(I32),
+                in_=w4_scales[:, 4 * quad : 4 * quad + 4, :].bitcast(I32),
+            )
 
         def first_product(half, stationary):
             bank = psum.tile([P, BANK], F32, name="bank")
-            cols = slice(half * BANK, (half + 1) * BANK)
             for a in range(2):
-                codes, scales = stationary(a)
+                codes, scales = stationary[a]
                 nc.tensor.matmul_mx(
                     out=bank[:],
                     lhsT=codes,
                     lhsT_scale=scales,
-                    rhs=v_words[a, half][:].bitcast(FP8X4),
-                    rhs_scale=v_sc[a][:, cols],
+                    rhs=v_words[a, half].bitcast(FP8X4),
+                    rhs_scale=v_sc[:, a, half * BANK : (half + 1) * BANK],
                     start=(a == 0),
                     stop=(a == 1),
                 )
@@ -182,53 +186,65 @@ def tile_list_antivenom_panel_features_kernel(
             else:
                 th = work.tile([P, S], F32, name="th", bufs=3)
             sn = work.tile([P, S], F32, name="sn", align_bytes=64)
-            rows = slice(P * i, P * (i + 1))
-            for half in range(2):
-                cols = slice(half * BANK, (half + 1) * BANK)
-                a1 = first_product(
-                    half,
-                    lambda a: (w1_codes[b][:, a, 2 * P * i : 2 * P * (i + 1)].bitcast(FP4X4), w1_sc[a][:, PASS * b + P * i : PASS * b + P * (i + 1)]),
+            place = P * i
+            w1_part = [
+                (
+                    w1_codes[b][:, a, 2 * place : 2 * (place + P)].bitcast(FP4X4),
+                    w1_sc[:, a, PASS * b + place : PASS * b + place + P],
                 )
-                nc.scalar.activation(out=th[:, cols], in_=a1[:], func=ACT.Tanh, bias=zero[:])
+                for a in range(2)
+            ]
+            w2_part = [
+                (w2_codes[a][b][:, place : place + P].bitcast(FP8X4), w2_sc[a][b][:, place : place + P])
+                for a in range(2)
+            ]
             for half in range(2):
-                cols = slice(half * BANK, (half + 1) * BANK)
-                a2 = first_product(half, lambda a: (w2_codes[a][b][:, rows].bitcast(FP8X4), w2_sc[a][b][:, rows]))
-                nc.scalar.activation(out=sn[:, cols], in_=a2[:], func=ACT.Sin, bias=zero[:], scale=0.5)
-            sq = held([P, S], F32, "first_sq") if (b, i) == (0, 0) else work.tile([P, S], F32, name="sq", bufs=3, align_bytes=64)
+                a1 = first_product(half, w1_part)
+                nc.scalar.activation(out=th[:, half * BANK : (half + 1) * BANK], in_=a1[:], func=ACT.Tanh, bias=zero[:])
+            for half in range(2):
+                a2 = first_product(half, w2_part)
+                nc.scalar.activation(
+                    out=sn[:, half * BANK : (half + 1) * BANK], in_=a2[:], func=ACT.Sin, bias=zero[:], scale=0.5
+                )
+            if (b, i) == (0, 0):
+                sq = held([P, S], F32, "first_sq")
+            else:
+                sq = work.tile([P, S], F32, name="sq", bufs=3, align_bytes=64)
             nc.scalar.activation(out=sq[:], in_=sn[:], func=ACT.Square, bias=zero[:])
             gi = g[:, b, i : i + 1]
-            h = work.tile([P, S], F32, name="h", bufs=2)
+            h = work.tile([P, S], F32, name="h")
             part = work.tile([P, S], F32, name="part", bufs=3)
-            if 4 * b + i < GAIN_ON_VECTOR:
+            if b == 0:
                 nc.vector.scalar_tensor_tensor(
                     out=part[:], in0=sq[:], scalar=-2.0, in1=th[:], op0=ALU.mult, op1=ALU.add
                 )
                 nc.vector.tensor_scalar(out=h[:], in0=part[:], scalar1=1.0, scalar2=gi, op0=ALU.add, op1=ALU.mult)
             else:
-                nc.scalar.activation(
-                    out=part[:], in_=sq[:], func=ACT.Identity, bias=gi, scale=g_neg2[:, b, i : i + 1]
-                )
+                nc.scalar.activation(out=part[:], in_=sq[:], func=ACT.Identity, bias=gi, scale=g_neg2[:, i : i + 1])
                 nc.vector.scalar_tensor_tensor(out=h[:], in0=th[:], scalar=gi, in1=part[:], op0=ALU.mult, op1=ALU.add)
             return h, sn, sq
 
-        def picked_tiles(width):
-            xa = work.tile([P, 4, width], F32, name="xa", bufs=1)
-            xb = work.tile([P, 4, width], F32, name="xb", bufs=1)
+        def picked_tiles():
+            xa = work.tile([P, 4, M], F32, name="xa", bufs=1)
+            xb = work.tile([P, 4, M], F32, name="xb", bufs=1)
             return xa, xb
 
         def pick(h, xa, xb, i, m0, width):
             cols = slice(m0 // 16, (m0 + width) // 16)
             for x, offsets, weight in ((xa, list_a, wa), (xb, list_b, wb)):
                 nc.vector.tensor_tensor(
-                    out=x[:, i, m0 : m0 + width], in0=h[:].indirect(offsets[:, cols]), in1=weight[:, m0 : m0 + width], op=ALU.mult
+                    out=x[:, i, m0 : m0 + width],
+                    in0=h[:].indirect(offsets[:, cols]),
+                    in1=weight[:, m0 : m0 + width],
+                    op=ALU.mult,
                 )
 
         def smaller(xa, xb, m0, width, name):
             z = keep.tile([P, width, 4], BF16, name=f"z{name}", align_bytes=64)
             nc.vector.tensor_tensor(
-                out=z[:].rearrange("p (c k) i -> p c i k", k=4),
-                in0=xa[:, :, m0 : m0 + width].rearrange("p i (c k) -> p c i k", k=4),
-                in1=xb[:, :, m0 : m0 + width].rearrange("p i (c k) -> p c i k", k=4),
+                out=z[:].rearrange("p (c u) i -> p c i u", u=4),
+                in0=xa[:, :, m0 : m0 + width].rearrange("p i (c u) -> p c i u", u=4),
+                in1=xb[:, :, m0 : m0 + width].rearrange("p i (c u) -> p c i u", u=4),
                 op=ALU.min,
             )
             codes = held([P, width], U32, f"z_codes{name}")
@@ -237,13 +253,13 @@ def tile_list_antivenom_panel_features_kernel(
             return codes, scales
 
         squares = []
-        xa, xb = picked_tiles(M)
+        xa, xb = picked_tiles()
         for i in range(4):
             h, sn, sq = features(0, i)
             squares.append(sq)
             pick(h, xa, xb, i, 0, M)
             if i == 1:
-                w1_codes.append(held([P, 2, 2 * PASS], U8, "first_sq")[:])
+                w1_codes.append(held([P, 2, 2 * PASS], U8, "first_sq"))
                 deal_w1(1)
             if i == 2:
                 grouped = squares[1][:].bitcast(BF16).rearrange("p (t q j) -> p t q j", t=4, j=4)
@@ -252,7 +268,7 @@ def tile_list_antivenom_panel_features_kernel(
         z0_codes, z0_sc = smaller(xa, xb, 0, M, "0")
 
         sines = []
-        xa, xb = picked_tiles(M)
+        xa, xb = picked_tiles()
         for i in range(4):
             h, sn, sq = features(1, i)
             sines.append(sn)
@@ -262,38 +278,36 @@ def tile_list_antivenom_panel_features_kernel(
 
         out_rows = out.rearrange("(c p) m -> p c m", p=P)
 
-        def second_product(c0, count, m0, width, z1, w_codes, w_sc):
+        def second_product(c0, count, width, z_parts, w_parts):
             bank = psum.tile([P, count, width], F32, name="bank")
-            z_ops = ((z0_codes[:, m0 : m0 + width], z0_sc[:, m0 : m0 + width]), (z1[0][:], z1[1][:]))
             for c in range(count):
                 cols = slice(P * (c0 + c), P * (c0 + c + 1))
                 for b in range(2):
                     nc.tensor.matmul_mx(
                         out=bank[:, c, :],
-                        lhsT=w_codes(b, cols).bitcast(FP8X4),
-                        lhsT_scale=w_sc(b, cols),
-                        rhs=z_ops[b][0].bitcast(FP8X4),
-                        rhs_scale=z_ops[b][1],
+                        lhsT=w_parts[b][0][:, cols].bitcast(FP8X4),
+                        lhsT_scale=w_parts[b][1][:, cols],
+                        rhs=z_parts[b][0].bitcast(FP8X4),
+                        rhs_scale=z_parts[b][1],
                         start=(b == 0),
                         stop=(b == 1),
                     )
             return bank
 
+        w3_parts = [(w3_codes[b][:], w3_sc[b][:]) for b in range(2)]
+        w4_parts = [(w4_codes[:, b, :], w4_sc[4 * b : P, :]) for b in range(2)]
         finished = []
-        for k, (m0, width) in enumerate(LAST_SLICES):
+        for number, (m0, width) in enumerate(OUT_SLICES):
             pick(h, xa, xb, 3, m0, width)
-            z1 = smaller(xa, xb, m0, width, f"1{k}")
-            if k == 0:
+            z1_codes, z1_sc = smaller(xa, xb, m0, width, f"1{number}")
+            if number == 0:
                 for b in range(2):
                     quantize(w3_codes[b][:], w3_sc[b][:], w3_rounded[b])
+            z_parts = ((z0_codes[:, m0 : m0 + width], z0_sc[:, m0 : m0 + width]), (z1_codes[:], z1_sc[:]))
             count = BANK // width
-            for c0 in range(0, 4, count):
-                y2 = second_product(
-                    c0, count, m0, width, z1, lambda b, cols: w4_codes[:, b, cols], lambda b, cols: w4_sc[4 * b : P, cols]
-                )
-                y1 = second_product(
-                    c0, count, m0, width, z1, lambda b, cols: w3_codes[b][:, cols], lambda b, cols: w3_sc[b][:, cols]
-                )
+            for c0 in range(0, N // P, count):
+                y2 = second_product(c0, count, width, z_parts, w4_parts)
+                y1 = second_product(c0, count, width, z_parts, w3_parts)
                 size = work.tile([P, count, width], F32, name="size")
                 damp = work.tile([P, count, width], F32, name="damp", bufs=4)
                 signed = work.tile([P, count, width], F32, name="signed", bufs=4)

from contextlib import ExitStack

import concourse.mybir as mybir

K, T, H, S, M, N = 1024, 2048, 1024, 1024, 512, 512
FLOPS = 2 * (2 * K * H * S + 2 * H * N * M)

F32 = mybir.dt.float32
BF16 = mybir.dt.bfloat16
I32 = mybir.dt.int32
U32 = mybir.dt.uint32
U16 = mybir.dt.uint16
U8 = mybir.dt.uint8
FP8X4 = mybir.dt.float8_e4m3fn_x4
FP4X4 = mybir.dt.float4_e2m1fn_x4
ALU = mybir.AluOpType
ACT = mybir.ActivationFunctionType

P = 128
PASS = 512
BANK = 512
OUT_SLICES = ((0, 128), (128, 256), (384, 128))


def tile_list_antivenom_panel_features_kernel(
    tc, tab_words, tab_scales, offs, offs2, offs3, w1_words, w1_scales, w2, gain, wga, wgb, w3, w4_words, w4_scales, out
):
    nc = tc.nc
    with ExitStack() as ctx:
        keep = ctx.enter_context(tc.tile_pool(name="keep", bufs=1))
        work = ctx.enter_context(tc.tile_pool(name="work", bufs=2))
        psum = ctx.enter_context(tc.psum_pool(name="psum", bufs=8))

        def held(shape, dtype, tag):
            return keep.tile(shape, dtype, name=tag, align_bytes=64)

        list_v = keep.tile([P, S // 16], U16, name="list_v")
        list_a = keep.tile([P, M // 16], U16, name="list_a")
        list_b = keep.tile([P, M // 16], U16, name="list_b")
        tab = [held([P, T], U32, f"tab{a}") for a in range(2)]
        tab_sc = held([P, T], U8, "tab_sc")
        picked_sc = held([P, S], U8, "picked_sc")
        v_sc = held([P, 2, S], U8, "v_sc")
        v_words = {}
        w1_raw = [held([P, 2, 2 * PASS], U8, "w1_raw0")]
        w1_codes = [held([P, 2, 2 * PASS], U8, "w1_codes0")]
        w1_sc_raw = held([P, 2, H], U8, "w1_sc_raw")
        w1_sc = held([P, 2, H], U8, "w1_sc")
        w2_codes = [[held([P, PASS], U32, f"w2_codes{a}{b}") for b in range(2)] for a in range(2)]
        w2_sc = [[held([P, PASS], U8, f"w2_sc{a}{b}") for b in range(2)] for a in range(2)]
        w3_codes = [held([P, N], U32, f"w3_codes{b}") for b in range(2)]
        w3_sc = [held([P, N], U8, f"w3_sc{b}") for b in range(2)]
        g = held([P, 2, 4], F32, "g")
        g_neg2 = held([P, 4], F32, "g_neg2")
        zero_in = held([P, 1], F32, "zero_in")
        zero = held([P, 1], F32, "zero")

        nc.vector.memset(w1_sc_raw[:].bitcast(I32), 0)
        nc.vector.memset(zero_in[:], 0.0)
        nc.scalar.activation(out=zero[:], in_=zero_in[:], func=ACT.Silu)
        for rows in (slice(32, 64), slice(64, P)):
            nc.vector.memset(tab_sc[rows, :].bitcast(I32), 0)
        nc.vector.memset(v_sc[:].bitcast(I32), 0)

        def load_rows(w, a, cols, raw):
            nc.sync.dma_start(out=raw[:], in_=w[PASS * a : PASS * (a + 1), cols].rearrange("(p j) c -> p j c", j=4))
            return raw

        def load_w1(b):
            src = w1_words[:, :, 2 * PASS * b : 2 * PASS * (b + 1)].rearrange("a p n -> p a n")
            nc.sync.dma_start(out=w1_raw[b][:].bitcast(I32), in_=src.bitcast(I32))

        def load_table(a):
            nc.sync.dma_start(out=tab[a][:].bitcast(I32), in_=tab_words[a].rearrange("p t i -> p (t i)").bitcast(I32))

        nc.sync.dma_start(out=tab_sc[0:32, :].bitcast(I32), in_=tab_scales.rearrange("a q t -> q a t").bitcast(I32))
        nc.sync.dma_start(list_v[:], offs)
        load_table(0)
        for quad in range(4):
            nc.sync.dma_start(
                out=w1_sc_raw[32 * quad : 32 * quad + 4, :, :].bitcast(I32),
                in_=w1_scales[:, 4 * quad : 4 * quad + 4, :].rearrange("a s n -> s a n").bitcast(I32),
            )
        load_table(1)
        load_w1(0)
        w2_raw = {(a, 0): load_rows(w2, a, slice(0, PASS), held([P, 4, PASS], F32, f"w2_first{a}")) for a in range(2)}
        nc.sync.dma_start(out=g[:], in_=gain.rearrange("(b p i) -> p b i", b=2, i=4))
        nc.sync.dma_start(list_a[:], offs2)
        nc.sync.dma_start(list_b[:], offs3)

        def deal_w1(b):
            nc.scalar.copy(
                out=w1_codes[b][:].bitcast(U16).rearrange("p a (t q) -> p a t q", t=4),
                in_=w1_raw[b][:].bitcast(U16).rearrange("p a (q t) -> p a t q", t=4),
            )

        def gather_words(a, half):
            cols = slice(half * BANK // 16, (half + 1) * BANK // 16)
            nc.vector.tensor_copy(out=v_words[a, half], in_=tab[a][:].indirect(list_v[:, cols]))

        def round_w2(copy, a, b, grouped):
            copy(
                out=grouped[:].rearrange("p t q j -> p q j t"),
                in_=w2_raw[a, b][:].rearrange("p j (q t) -> p q j t", t=4),
            )
            return grouped[:].rearrange("p t q j -> p (t q j)")

        def round_w3(b, spent):
            grouped = spent[:].bitcast(BF16).rearrange("p (c j) -> p c j", j=4)
            nc.scalar.copy(
                out=grouped[:].rearrange("p (c u) j -> p c j u", u=4),
                in_=w3_raw[b][:].rearrange("p j (c u) -> p c j u", u=4),
            )
            return grouped[:].rearrange("p c j -> p (c j)")

        def quantize(codes, scales, values):
            nc.vector.quantize_mx(out=codes.bitcast(FP8X4), scales=scales, in_=values)

        def staged(number):
            return held([P, 4, P, 4], BF16, f"staged{number}")

        deal_w1(0)
        w2_rounded = [round_w2(nc.scalar.copy, 0, 0, staged(0))]
        nc.vector.tensor_copy(out=picked_sc[:], in_=tab_sc[:].indirect(list_v[:]))
        for quad in range(4):
            nc.sync.dma_start(
                out=v_sc[32 * quad : 32 * quad + 4, :, :].bitcast(I32),
                in_=picked_sc[8 * quad : 8 * quad + 8, :].bitcast(I32),
            )
        first_words = held([P, 2, BANK], U32, "tab_sc")
        for half in range(2):
            v_words[0, half] = first_words[:, half, :]
            gather_words(0, half)
        nc.vector.tensor_copy(
            out=w1_sc[:].rearrange("p a (b t q) -> p (a b) t q", b=2, t=4),
            in_=w1_sc_raw[:].rearrange("p a (b q t) -> p (a b) t q", b=2, t=4),
        )
        second_words = held([P, 2, BANK], U32, "w1_sc_raw")
        for half in range(2):
            v_words[1, half] = second_words[:, half, :]
            gather_words(1, half)

        w2_raw[0, 1] = load_rows(w2, 0, slice(PASS, 2 * PASS), held([P, 4, PASS], F32, "tab0"))
        weights = held([P, 2, M], F32, "tab1")
        wa, wb = weights[:, 0, :], weights[:, 1, :]
        nc.sync.dma_start(out=wa, in_=wga)
        nc.sync.dma_start(out=wb, in_=wgb)
        w2_rounded.append(round_w2(nc.vector.tensor_copy, 1, 0, staged(1)))
        for c0, c1 in ((0, P), (P, PASS)):
            for a in range(2):
                quantize(w2_codes[a][0][:, c0:c1], w2_sc[a][0][:, c0:c1], w2_rounded[a][:, 4 * c0 : 4 * c1])
        quantize(w2_codes[0][1][:], w2_sc[0][1][:], round_w2(nc.vector.tensor_copy, 0, 1, staged(2)))
        nc.vector.tensor_scalar(out=g_neg2[:], in0=g[:, 1, :], scalar1=-2.0, scalar2=None, op0=ALU.mult)
        w1_raw.append(held([P, 2, 2 * PASS], U8, "staged1"))
        load_w1(1)
        w2_raw[1, 1] = load_rows(w2, 1, slice(PASS, 2 * PASS), held([P, 4, PASS], F32, "staged0"))
        w3_raw = [load_rows(w3, 0, slice(0, N), held([P, 4, N], F32, "tab0"))]
        w4_codes = held([P, 2, N], U32, "staged2")
        nc.sync.dma_start(out=w4_codes[:].bitcast(I32), in_=w4_words.rearrange("a p c i -> p a (c i)").bitcast(I32))
        w4_sc = held([P, N], U8, "picked_sc")
        nc.gpsimd.memset(w4_sc[:].bitcast(I32), 0)
        for quad in range(4):
            nc.sync.dma_start(
                out=w4_sc[32 * quad : 32 * quad + 8, :].bitcast(I32),
                in_=w4_scales[:, 4 * quad : 4 * quad + 4, :].bitcast(I32),
            )

        def first_product(half, stationary):
            bank = psum.tile([P, BANK], F32, name="bank")
            for a in range(2):
                codes, scales = stationary[a]
                nc.tensor.matmul_mx(
                    out=bank[:],
                    lhsT=codes,
                    lhsT_scale=scales,
                    rhs=v_words[a, half].bitcast(FP8X4),
                    rhs_scale=v_sc[:, a, half * BANK : (half + 1) * BANK],
                    start=(a == 0),
                    stop=(a == 1),
                )
            return bank

        def features(b, i):
            if b == 0:
                th = w2_raw[i // 2, 0][:].rearrange("p (u j) c -> p u (j c)", u=2)[:, i % 2, :]
            else:
                th = work.tile([P, S], F32, name="th", bufs=3)
            sn = work.tile([P, S], F32, name="sn", align_bytes=64)
            place = P * i
            w1_part = [
                (
                    w1_codes[b][:, a, 2 * place : 2 * (place + P)].bitcast(FP4X4),
                    w1_sc[:, a, PASS * b + place : PASS * b + place + P],
                )
                for a in range(2)
            ]
            w2_part = [
                (w2_codes[a][b][:, place : place + P].bitcast(FP8X4), w2_sc[a][b][:, place : place + P])
                for a in range(2)
            ]
            for half in range(2):
                a1 = first_product(half, w1_part)
                nc.scalar.activation(out=th[:, half * BANK : (half + 1) * BANK], in_=a1[:], func=ACT.Tanh, bias=zero[:])
            for half in range(2):
                a2 = first_product(half, w2_part)
                nc.scalar.activation(
                    out=sn[:, half * BANK : (half + 1) * BANK], in_=a2[:], func=ACT.Sin, bias=zero[:], scale=0.5
                )
            if (b, i) == (0, 0):
                sq = held([P, S], F32, "first_sq")
            else:
                sq = work.tile([P, S], F32, name="sq", bufs=3, align_bytes=64)
            nc.scalar.activation(out=sq[:], in_=sn[:], func=ACT.Square, bias=zero[:])
            gi = g[:, b, i : i + 1]
            h = work.tile([P, S], F32, name="h")
            part = work.tile([P, S], F32, name="part", bufs=3)
            if b == 0:
                nc.vector.scalar_tensor_tensor(
                    out=part[:], in0=sq[:], scalar=-2.0, in1=th[:], op0=ALU.mult, op1=ALU.add
                )
                nc.vector.tensor_scalar(out=h[:], in0=part[:], scalar1=1.0, scalar2=gi, op0=ALU.add, op1=ALU.mult)
            else:
                nc.scalar.activation(out=part[:], in_=sq[:], func=ACT.Identity, bias=gi, scale=g_neg2[:, i : i + 1])
                nc.vector.scalar_tensor_tensor(out=h[:], in0=th[:], scalar=gi, in1=part[:], op0=ALU.mult, op1=ALU.add)
            return h, sn, sq

        def picked_tiles():
            xa = work.tile([P, 4, M], F32, name="xa", bufs=1)
            xb = work.tile([P, 4, M], F32, name="xb", bufs=1)
            return xa, xb

        def pick(h, xa, xb, i, m0, width):
            cols = slice(m0 // 16, (m0 + width) // 16)
            for x, offsets, weight in ((xa, list_a, wa), (xb, list_b, wb)):
                nc.vector.tensor_tensor(
                    out=x[:, i, m0 : m0 + width],
                    in0=h[:].indirect(offsets[:, cols]),
                    in1=weight[:, m0 : m0 + width],
                    op=ALU.mult,
                )

        def smaller(xa, xb, m0, width, name):
            z = keep.tile([P, width, 4], BF16, name=f"z{name}", align_bytes=64)
            nc.vector.tensor_tensor(
                out=z[:].rearrange("p (c u) i -> p c i u", u=4),
                in0=xa[:, :, m0 : m0 + width].rearrange("p i (c u) -> p c i u", u=4),
                in1=xb[:, :, m0 : m0 + width].rearrange("p i (c u) -> p c i u", u=4),
                op=ALU.min,
            )
            codes = held([P, width], U32, f"z_codes{name}")
            scales = held([P, width], U8, f"z_sc{name}")
            quantize(codes[:], scales[:], z[:].rearrange("p m i -> p (m i)"))
            return codes, scales

        squares = []
        xa, xb = picked_tiles()
        for i in range(4):
            h, sn, sq = features(0, i)
            squares.append(sq)
            pick(h, xa, xb, i, 0, M)
            if i == 1:
                w1_codes.append(held([P, 2, 2 * PASS], U8, "first_sq"))
                deal_w1(1)
            if i == 2:
                grouped = squares[1][:].bitcast(BF16).rearrange("p (t q j) -> p t q j", t=4, j=4)
                quantize(w2_codes[1][1][:], w2_sc[1][1][:], round_w2(nc.scalar.copy, 1, 1, grouped))
                w3_raw.append(load_rows(w3, 1, slice(0, N), held([P, 4, N], F32, "staged0")))
        z0_codes, z0_sc = smaller(xa, xb, 0, M, "0")

        sines = []
        xa, xb = picked_tiles()
        for i in range(4):
            h, sn, sq = features(1, i)
            sines.append(sn)
            if i < 3:
                pick(h, xa, xb, i, 0, M)
        w3_rounded = [round_w3(b, sines[2 + b]) for b in range(2)]

        out_rows = out.rearrange("(c p) m -> p c m", p=P)

        def second_product(c0, count, width, z_parts, w_parts):
            bank = psum.tile([P, count, width], F32, name="bank")
            for c in range(count):
                cols = slice(P * (c0 + c), P * (c0 + c + 1))
                for b in range(2):
                    nc.tensor.matmul_mx(
                        out=bank[:, c, :],
                        lhsT=w_parts[b][0][:, cols].bitcast(FP8X4),
                        lhsT_scale=w_parts[b][1][:, cols],
                        rhs=z_parts[b][0].bitcast(FP8X4),
                        rhs_scale=z_parts[b][1],
                        start=(b == 0),
                        stop=(b == 1),
                    )
            return bank

        w3_parts = [(w3_codes[b][:], w3_sc[b][:]) for b in range(2)]
        w4_parts = [(w4_codes[:, b, :], w4_sc[4 * b : P, :]) for b in range(2)]
        finished = []
        for number, (m0, width) in enumerate(OUT_SLICES):
            pick(h, xa, xb, 3, m0, width)
            z1_codes, z1_sc = smaller(xa, xb, m0, width, f"1{number}")
            if number == 0:
                for b in range(2):
                    quantize(w3_codes[b][:], w3_sc[b][:], w3_rounded[b])
            z_parts = ((z0_codes[:, m0 : m0 + width], z0_sc[:, m0 : m0 + width]), (z1_codes[:], z1_sc[:]))
            count = BANK // width
            for c0 in range(0, N // P, count):
                y2 = second_product(c0, count, width, z_parts, w4_parts)
                y1 = second_product(c0, count, width, z_parts, w3_parts)
                size = work.tile([P, count, width], F32, name="size")
                damp = work.tile([P, count, width], F32, name="damp", bufs=4)
                signed = work.tile([P, count, width], F32, name="signed", bufs=4)
                nc.scalar.activation(out=size[:], in_=y2[:], func=ACT.Abs, bias=zero[:])
                nc.scalar.activation(out=damp[:], in_=size[:], func=ACT.Exp, bias=zero[:], scale=-1.0)
                nc.scalar.activation(out=signed[:], in_=y1[:], func=ACT.Tanh, bias=zero[:])
                finished.append((c0, count, m0, width, signed, damp))
        for c0, count, m0, width, signed, damp in finished:
            result = work.tile([P, count, width], F32, name="result", bufs=4)
            nc.vector.tensor_tensor(out=result[:], in0=signed[:], in1=damp[:], op=ALU.mult)
            nc.sync.dma_start(out=out_rows[:, c0 : c0 + count, m0 : m0 + width], in_=result[:])
